import numpy as np
import ml_dtypes


def mxq(x, axis, fmt="e4m3"):
    dtype, down = {"e4m3": (ml_dtypes.float8_e4m3fn, 7), "e5m2": (ml_dtypes.float8_e5m2, 14)}[fmt]
    v = np.moveaxis(np.asarray(x, np.float32).astype(ml_dtypes.bfloat16).astype(np.float64), axis, -1)
    blocks = v.reshape(v.shape[:-1] + (-1, 32))
    amax = np.abs(blocks).max(-1, keepdims=True)
    byte = np.maximum(np.where(amax > 0, np.frexp(amax)[1] - 1 + 127, 0) - down, 1)
    scale = np.exp2(byte - 127.0)
    codes = (blocks / scale).astype(np.float32).astype(dtype).astype(np.float64)
    return np.moveaxis((codes * scale).reshape(v.shape), -1, axis)


WIDE = False


def mx_kscale(k):
    if not WIDE:
        return np.ones(k)
    levels = np.array([10, -10, 5, -5, 0])
    if k % 512:
        return np.exp2(np.random.permutation(np.resize(levels, k // 32))).repeat(32)
    a = np.empty((k // 512, 16))
    for p in range(k // 512):
        a[p, :8] = np.random.permutation(np.resize(levels, 8))
        for g in range(8):
            far = levels[np.abs(levels - a[p, g]) >= 10]
            a[p, g + 8] = far[np.random.randint(len(far))]
    return np.exp2(a.ravel()).repeat(32)


def f64(x):
    return np.asarray(x).astype(np.float64)


def striped(idx):
    return np.tile(idx.reshape(-1, 16).T, (8, 1)).astype(np.uint16)


def unstriped(offs):
    return offs[:16].T.reshape(-1).astype(np.int64)


def striped8(idx):
    return np.concatenate([x.reshape(-1, 16).T for x in idx]).astype(np.uint16)


def runs(offs, k):
    lists = np.stack([offs[16 * r : 16 * r + 16].T.reshape(-1) for r in range(8)]).astype(np.int64)
    return lists[np.arange(k) % 512 // 64]


def pack_weight(w):
    k, n = w.shape
    w = f64(np.asarray(w, np.float32).astype(ml_dtypes.bfloat16)).reshape(k // 32, 32, n)
    amax = np.abs(w).max(1)
    byte = np.clip(np.where(amax > 0, np.frexp(amax)[1] - 1 + 127 - 7, 1), 1, 254)
    scaled = (w * np.exp2(127.0 - byte)[:, None, :]).reshape(k, n).astype(np.float32)
    words = np.ascontiguousarray(scaled.reshape(k // 512, 128, 4, n).transpose(0, 1, 3, 2)).astype(ml_dtypes.float8_e4m3fn).view(np.uint8)
    return words, np.ascontiguousarray(byte.astype(np.uint8).reshape(k // 512, 16, n))


def unpack_weight(words, scales):
    g, p, n, _ = words.shape
    vals = np.ascontiguousarray(words).view(ml_dtypes.float8_e4m3fn).astype(np.float64) * np.repeat(np.exp2(scales.astype(np.float64) - 127.0), 8, axis=1)[..., None]
    return vals.transpose(0, 1, 3, 2).reshape(g * 512, n)


def sigmoid(v):
    return 1.0 / (1.0 + np.exp(-np.maximum(v, -700.0)))


K, T, S, N, H, G = 512, 2048, 256, 512, 512, 2048


def setup_inputs():
    n = np.random.standard_normal
    s = mx_kscale(K)[:, None]
    u = mx_kscale(K)
    packed_xT = pack_weight(n((K, T)) * s)
    packed_dT = pack_weight(n((K, G)) / s)
    return {
        "x_words": packed_xT[0],
        "x_scales": packed_xT[1],
        "w1": (n((K, H)) / np.sqrt(K) / s).astype(np.float32),
        "gn": (np.random.uniform(0.5, 1.5, (H, 1)) * u[:, None]).astype(np.float32),
        "w2": (n((H, N)) / np.sqrt(H) / u[:, None]).astype(np.float32),
        "d_words": packed_dT[0],
        "d_scales": packed_dT[1],
        "offs": striped(np.random.permutation(T)[:S]),
        "n1": striped8(np.stack([np.random.permutation(S) for _ in range(8)])),
        "n2": striped8(np.stack([np.random.permutation(S) for _ in range(8)])),
        "two": striped(np.random.permutation(T)[:S]),
        "k1": striped8(np.random.randint(0, G, (8, H))),
        "n3": striped(np.random.permutation(S)),
        "n4": striped(np.random.permutation(S)),
    }


def reference(x_words, x_scales, w1, gn, w2, d_words, d_scales, offs, n1, n2, two, k1, n3, n4):
    xq = unpack_weight(x_words, x_scales)[:, unstriped(offs)]
    y = mxq(f64(w1), 0, "e4m3").T @ xq
    st = y + y[np.arange(H)[:, None], runs(n1, H)]
    z = f64(gn) * (st * (np.tanh(st[np.arange(H)[:, None], runs(n2, H)])))
    a = mxq(f64(w2), 0, "e4m3").T @ mxq(z, 0, "e4m3")
    d_k1 = unpack_weight(d_words, d_scales)[np.arange(K)[:, None], runs(k1, K)]
    x_two = unpack_weight(x_words, x_scales)[:, unstriped(two)]
    b = 0.0625 * (d_k1.T @ x_two)
    return a * (sigmoid(b[:, unstriped(n4)])) - (0.5 * a[:, unstriped(n3)])

@@ -1,0 +1,199 @@
+from contextlib import ExitStack
+
+import concourse.mybir as mybir
+
+K, T, S, N, H, G = 512, 2048, 256, 512, 512, 2048
+FLOPS = 2 * K * H * S + 2 * H * N * S + 2 * K * H * S
+
+F32 = mybir.dt.float32
+BF16 = mybir.dt.bfloat16
+I32 = mybir.dt.int32
+U32 = mybir.dt.uint32
+U16 = mybir.dt.uint16
+U8 = mybir.dt.uint8
+FP8X4 = mybir.dt.float8_e4m3fn_x4
+ACT = mybir.ActivationFunctionType
+ALU = mybir.AluOpType
+
+P = 128
+PACK = 4
+TILES = 4
+HALF = S // 2
+FUSED_HALVES = 3
+
+
+def tile_picked_cdjoingatebhopp_none_p_kernel(
+    tc, x_words, x_scales, w1, gn, w2, d_words, d_scales, offs, n1, n2, two, k1, n3, n4, out
+):
+    nc = tc.nc
+    with ExitStack() as ctx:
+        keep = ctx.enter_context(tc.tile_pool(name="keep", bufs=1))
+        psum = ctx.enter_context(tc.psum_pool(name="psum", bufs=1))
+
+        def load_list(src, name):
+            tile = keep.tile(list(src.shape), U16, name=name)
+            nc.sync.dma_start(tile[:], src)
+            return tile
+
+        def half_of(tile, h):
+            return tile[:, h * (HALF // 16) : (h + 1) * (HALF // 16)]
+
+        def cols(h):
+            return slice(h * HALF, (h + 1) * HALF)
+
+        def block(t):
+            return slice(t * P, (t + 1) * P)
+
+        xs_win = keep.tile([P, T], U8, name="xs_win", tag="x_side", align_bytes=64)
+        ds_win = keep.tile([P, G], U8, name="ds_win", tag="d_side", align_bytes=64)
+        nc.gpsimd.memset(xs_win[:].bitcast(I32), 0)
+        nc.vector.memset(ds_win[:].bitcast(I32), 0)
+        nc.gpsimd.dma_start(xs_win[0:P:8, :].bitcast(I32), x_scales[0].bitcast(I32))
+        nc.gpsimd.dma_start(ds_win[0:P:8, :].bitcast(I32), d_scales[0].bitcast(I32))
+        gn_sb = keep.tile([P, TILES], F32, name="gn_sb")
+        nc.gpsimd.dma_start(gn_sb[:], gn.rearrange("(p t) o -> p (t o)", t=TILES))
+
+        offs_sb = load_list(offs, "offs_sb")
+        w1_raw = keep.tile([P, PACK, H], F32, name="w1_raw", tag="w_raw", align_bytes=64)
+        nc.sync.dma_start(w1_raw[:], w1.rearrange("(p j) c -> p j c", j=PACK))
+        two_sb = load_list(two, "two_sb")
+        k1_sb = load_list(k1, "k1_sb")
+        n1_sb = load_list(n1, "n1_sb")
+        xw_win = keep.tile([P, T], U32, name="xw_win", tag="words", align_bytes=64)
+        nc.sync.dma_start(xw_win[:].bitcast(I32), x_words[0].rearrange("p n r -> p (n r)").bitcast(I32))
+        n2_sb = load_list(n2, "n2_sb")
+        n4_sb = load_list(n4, "n4_sb")
+        n3_sb = load_list(n3, "n3_sb")
+
+        def place_scales(got, name):
+            plane = keep.tile(list(got.shape), U8, name=name, align_bytes=64)
+            nc.vector.tensor_copy(plane[:].bitcast(I32), got[:].bitcast(I32))
+            for r in range(1, 4):
+                nc.sync.dma_start(plane[r:P:32, :].bitcast(I32), got[8 * r : P : 32, :].bitcast(I32))
+            return plane
+
+        one_got = keep.tile([P, S], U8, name="one_got")
+        nc.vector.tensor_copy(one_got[:], xs_win[:].indirect(offs_sb[:]))
+        one_s = place_scales(one_got, "one_s")
+        b_got = keep.tile([P, S + H], U8, name="b_got")
+        nc.vector.tensor_copy(b_got[:, 0:S], xs_win[:].indirect(two_sb[:]))
+        nc.vector.tensor_copy(b_got[:, S:], ds_win[:].indirect(k1_sb[:]))
+        b_s = place_scales(b_got, "b_s")
+
+        w1_bf = keep.tile([P, TILES, P, PACK], BF16, name="w1_bf", tag="w_bf", align_bytes=64)
+        nc.scalar.copy(
+            w1_bf[:].rearrange("p t m j -> p m j t"), w1_raw[:].rearrange("p j (m t) -> p m j t", t=TILES)
+        )
+        w1_q = keep.tile([P, H], U32, name="w1_q", tag="x_side", align_bytes=64)
+        w1_s = keep.tile([P, H], U8, name="w1_s", align_bytes=64)
+        for u in range(2):
+            pair = slice(2 * u * P, 2 * (u + 1) * P)
+            nc.vector.quantize_mx(
+                w1_q[:, pair].bitcast(FP8X4), w1_s[:, pair],
+                w1_bf[:, 2 * u : 2 * u + 2].rearrange("p t m j -> p (t m j)"),
+            )
+
+        w2_raw = keep.tile([P, PACK, N], F32, name="w2_raw", tag="w_raw", align_bytes=64)
+        nc.sync.dma_start(w2_raw[:], w2.rearrange("(p j) c -> p j c", j=PACK))
+
+        x_one = keep.tile([P, S], U32, name="x_one", tag="d_side", align_bytes=64)
+        x_two = keep.tile([P, S], U32, name="x_two", align_bytes=64)
+        nc.vector.tensor_copy(x_one[:], xw_win[:].indirect(offs_sb[:]))
+        nc.vector.tensor_copy(x_two[:], xw_win[:].indirect(two_sb[:]))
+        dw_win = keep.tile([P, G], U32, name="dw_win", tag="words", align_bytes=64)
+        nc.sync.dma_start(dw_win[:].bitcast(I32), d_words[0].rearrange("p n r -> p (n r)").bitcast(I32))
+
+        y_ps, y_sb, y_got, st, th = [], [], [], [], []
+        for t in range(TILES):
+            y_ps.append(psum.tile([P, S], F32, name=f"y_ps{t}", tag=f"bank{t}"))
+            nc.tensor.matmul_mx(
+                y_ps[t][:], lhsT=w1_q[:, block(t)].bitcast(FP8X4), lhsT_scale=w1_s[:, block(t)],
+                rhs=x_one[:].bitcast(FP8X4), rhs_scale=one_s[:], start=True, stop=True,
+            )
+            y_sb.append(keep.tile([P, S], F32, name=f"y_sb{t}"))
+            if t == 0:
+                nc.scalar.copy(y_sb[t][:], y_ps[t][:])
+            else:
+                nc.vector.tensor_copy(y_sb[t][:], y_ps[t][:])
+        for t in range(TILES):
+            y_got.append(keep.tile([P, S], F32, name=f"y_got{t}"))
+            for h in range(2):
+                nc.scalar.activation(y_got[t][:, cols(h)], y_sb[t][:].indirect(half_of(n1_sb, h)), ACT.Copy)
+            st.append(keep.tile([P, S], F32, name=f"st{t}"))
+            nc.vector.tensor_tensor(st[t][:], y_ps[t][:], y_got[t][:], ALU.add)
+        for t in range(TILES):
+            th.append(keep.tile([P, S], F32, name=f"th{t}"))
+            nc.scalar.activation(th[t][:], st[t][:], ACT.Tanh)
+
+        w2_bf = keep.tile([P, N, PACK], BF16, name="w2_bf", tag="w_bf", align_bytes=64)
+        nc.vector.tensor_copy(
+            w2_bf[:].rearrange("p (c i) j -> p c j i", i=4), w2_raw[:].rearrange("p j (c i) -> p c j i", i=4)
+        )
+        w2_q = keep.tile([P, N], U32, name="w2_q", align_bytes=64)
+        w2_s = keep.tile([P, N], U8, name="w2_s", align_bytes=64)
+        nc.vector.quantize_mx(w2_q[:].bitcast(FP8X4), w2_s[:], w2_bf[:].rearrange("p c j -> p (c j)"))
+
+        d_got = keep.tile([P, H], U32, name="d_got", tag="w_bf", align_bytes=64)
+        nc.vector.tensor_copy(d_got[:], dw_win[:].indirect(k1_sb[:]))
+        b_ps = []
+        for t in range(TILES):
+            b_ps.append(psum.tile([P, S], F32, name=f"b_ps{t}", tag=f"bank{TILES + t}"))
+            nc.tensor.matmul_mx(
+                b_ps[t][:], lhsT=d_got[:, block(t)].bitcast(FP8X4),
+                lhsT_scale=b_s[:, S + t * P : S + (t + 1) * P],
+                rhs=x_two[:].bitcast(FP8X4), rhs_scale=b_s[:, 0:S], start=True, stop=True,
+            )
+
+        a_ps = [psum.tile([P, S], F32, name=f"a_ps{t}", tag=f"bank{t}") for t in range(TILES)]
+        for h in range(2):
+            th_got = keep.tile([P, TILES, HALF], F32, name=f"th_got{h}")
+            z_rows = keep.tile([P, TILES, HALF], BF16, name=f"z_rows{h}", tag=("words", "w_raw")[h], align_bytes=64)
+            for t in range(TILES):
+                nc.scalar.activation(th_got[:, t, :], th[t][:].indirect(half_of(n2_sb, h)), ACT.Copy)
+                nc.vector.scalar_tensor_tensor(
+                    z_rows[:, t, :], st[t][:, cols(h)], gn_sb[:, t : t + 1], th_got[:, t, :], ALU.mult, ALU.mult
+                )
+            z_bf = keep.tile([P, HALF, PACK], BF16, name=f"z_bf{h}", align_bytes=64)
+            nc.vector.tensor_copy(
+                z_bf[:].rearrange("p (c i) t -> p c t i", i=4), z_rows[:].rearrange("p t (c i) -> p c t i", i=4)
+            )
+            z_q = keep.tile([P, HALF], U32, name=f"z_q{h}", align_bytes=64)
+            z_s = keep.tile([P, HALF], U8, name=f"z_s{h}", align_bytes=64)
+            nc.vector.quantize_mx(z_q[:].bitcast(FP8X4), z_s[:], z_bf[:].rearrange("p c t -> p (c t)"))
+            for t in range(TILES):
+                nc.tensor.matmul_mx(
+                    a_ps[t][:, cols(h)], lhsT=w2_q[:, block(t)].bitcast(FP8X4), lhsT_scale=w2_s[:, block(t)],
+                    rhs=z_q[:].bitcast(FP8X4), rhs_scale=z_s[:], start=True, stop=True,
+                )
+
+        gate = []
+        tb = []
+        for t in range(TILES):
+            tb.append(keep.tile([P, S], F32, name=f"tb{t}"))
+            nc.scalar.activation(tb[t][:], b_ps[t][:], ACT.Tanh, scale=0.0625 * 0.5)
+        for t in range(TILES):
+            gate.append(keep.tile([P, S], F32, name=f"gate{t}"))
+            for h in range(2):
+                nc.scalar.activation(gate[t][:, cols(h)], tb[t][:].indirect(half_of(n4_sb, h)), ACT.Copy)
+
+        nhs = []
+        for t in range(TILES):
+            nhs.append(keep.tile([P, S], F32, name=f"nh{t}"))
+            nc.vector.tensor_scalar(nhs[t][:], a_ps[t][:], -0.5, None, ALU.mult)
+        for t in range(TILES):
+            nh = nhs[t]
+            prod = keep.tile([P, S], F32, name=f"prod{t}")
+            nc.vector.scalar_tensor_tensor(prod[:], gate[t][:], 1.0, nh[:], ALU.add, ALU.mult)
+            res = keep.tile([P, S], F32, name=f"res{t}")
+            got = keep.tile([P, S], F32, name=f"a_got{t}")
+            fused = min(max(FUSED_HALVES - 2 * t, 0), 2)
+            for h in range(fused):
+                nc.vector.tensor_tensor(
+                    res[:, cols(h)], nh[:].indirect(half_of(n3_sb, h)), prod[:, cols(h)], ALU.subtract
+                )
+            for h in range(fused, 2):
+                nc.scalar.activation(got[:, cols(h)], nh[:].indirect(half_of(n3_sb, h)), ACT.Copy)
+            if fused < 2:
+                rest = slice(fused * HALF, S)
+                nc.vector.tensor_tensor(res[:, rest], got[:, rest], prod[:, rest], ALU.subtract)
+            nc.sync.dma_start(out[block(t), :], res[:])

@@ -18,8 +18,8 @@ ALU = mybir.AluOpType
 P = 128
 PACK = 4
 TILES = 4
-HALF = S // 2
-FUSED_HALVES = 3
+FUSED_TILES = 1
+CAST_SPLIT = 56
 
 
 def tile_picked_cdjoingatebhopp_none_p_kernel(
@@ -35,38 +35,39 @@ def tile_picked_cdjoingatebhopp_none_p_kernel(
             nc.sync.dma_start(tile[:], src)
             return tile
 
-        def half_of(tile, h):
-            return tile[:, h * (HALF // 16) : (h + 1) * (HALF // 16)]
-
-        def cols(h):
-            return slice(h * HALF, (h + 1) * HALF)
-
         def block(t):
             return slice(t * P, (t + 1) * P)
 
+        def as_words(packed):
+            return packed[0].rearrange("p n r -> p (n r)").bitcast(I32)
+
         xs_win = keep.tile([P, T], U8, name="xs_win", tag="x_side", align_bytes=64)
         ds_win = keep.tile([P, G], U8, name="ds_win", tag="d_side", align_bytes=64)
-        nc.gpsimd.memset(xs_win[:].bitcast(I32), 0)
-        nc.vector.memset(ds_win[:].bitcast(I32), 0)
-        nc.gpsimd.dma_start(xs_win[0:P:8, :].bitcast(I32), x_scales[0].bitcast(I32))
-        nc.gpsimd.dma_start(ds_win[0:P:8, :].bitcast(I32), d_scales[0].bitcast(I32))
-        gn_sb = keep.tile([P, TILES], F32, name="gn_sb")
-        nc.gpsimd.dma_start(gn_sb[:], gn.rearrange("(p t) o -> p (t o)", t=TILES))
+        nc.vector.memset(xs_win[:].bitcast(I32), 0)
+        nc.gpsimd.memset(ds_win[:].bitcast(I32), 0)
+        rows = [keep.tile([P, 3 * S], F32, name=f"rows{t}") for t in range(TILES)]
+        for t in range(TILES - 1):
+            nc.gpsimd.memset(rows[t][:, S:], 0.0)
+        nc.scalar.copy(rows[TILES - 1][:, S:], rows[0][:, S:])
 
         offs_sb = load_list(offs, "offs_sb")
-        w1_raw = keep.tile([P, PACK, H], F32, name="w1_raw", tag="w_raw", align_bytes=64)
-        nc.sync.dma_start(w1_raw[:], w1.rearrange("(p j) c -> p j c", j=PACK))
+        w1_raw = keep.tile([P, PACK, H], F32, name="w1_raw")
+        w1_rows = w1.rearrange("(p j) c -> p j c", j=PACK)
+        nc.sync.dma_start(w1_raw[:, 0:2, :], w1_rows[:, 0:2, :])
+        nc.sync.dma_start(xs_win[0:P:8, :].bitcast(I32), x_scales[0].bitcast(I32))
+        nc.sync.dma_start(ds_win[0:P:8, :].bitcast(I32), d_scales[0].bitcast(I32))
         two_sb = load_list(two, "two_sb")
         k1_sb = load_list(k1, "k1_sb")
         n1_sb = load_list(n1, "n1_sb")
-        xw_win = keep.tile([P, T], U32, name="xw_win", tag="words", align_bytes=64)
-        nc.sync.dma_start(xw_win[:].bitcast(I32), x_words[0].rearrange("p n r -> p (n r)").bitcast(I32))
+        nc.sync.dma_start(w1_raw[:, 2:4, :], w1_rows[:, 2:4, :])
+        xw_win = keep.tile([P, T], U32, name="xw_win", tag="words")
+        nc.sync.dma_start(xw_win[:].bitcast(I32), as_words(x_words))
         n2_sb = load_list(n2, "n2_sb")
         n4_sb = load_list(n4, "n4_sb")
         n3_sb = load_list(n3, "n3_sb")
 
-        def place_scales(got, name):
-            plane = keep.tile(list(got.shape), U8, name=name, align_bytes=64)
+        def place_scales(got, name, tag):
+            plane = keep.tile(list(got.shape), U8, name=name, tag=tag, align_bytes=64)
             nc.vector.tensor_copy(plane[:].bitcast(I32), got[:].bitcast(I32))
             for r in range(1, 4):
                 nc.sync.dma_start(plane[r:P:32, :].bitcast(I32), got[8 * r : P : 32, :].bitcast(I32))
@@ -74,56 +75,70 @@ def tile_picked_cdjoingatebhopp_none_p_kernel(
 
         one_got = keep.tile([P, S], U8, name="one_got")
         nc.vector.tensor_copy(one_got[:], xs_win[:].indirect(offs_sb[:]))
-        one_s = place_scales(one_got, "one_s")
+        one_s = place_scales(one_got, "one_s", "one_s")
         b_got = keep.tile([P, S + H], U8, name="b_got")
         nc.vector.tensor_copy(b_got[:, 0:S], xs_win[:].indirect(two_sb[:]))
-        nc.vector.tensor_copy(b_got[:, S:], ds_win[:].indirect(k1_sb[:]))
-        b_s = place_scales(b_got, "b_s")
 
-        w1_bf = keep.tile([P, TILES, P, PACK], BF16, name="w1_bf", tag="w_bf", align_bytes=64)
-        nc.scalar.copy(
-            w1_bf[:].rearrange("p t m j -> p m j t"), w1_raw[:].rearrange("p j (m t) -> p m j t", t=TILES)
-        )
-        w1_q = keep.tile([P, H], U32, name="w1_q", tag="x_side", align_bytes=64)
+        dw_win = keep.tile([P, G], U32, name="dw_win", tag="x_side", align_bytes=64)
+        nc.sync.dma_start(dw_win[:].bitcast(I32), as_words(d_words))
+
+        nc.vector.tensor_copy(b_got[:, S:], ds_win[:].indirect(k1_sb[:]))
+        w1_bf = keep.tile([P, TILES, P, PACK], BF16, name="w1_bf", tag="w1_bf", align_bytes=64)
+        src = w1_raw[:].rearrange("p j (m t) -> p m t j", t=TILES)
+        dst = w1_bf[:].rearrange("p t m j -> p m t j")
+        nc.scalar.copy(dst[:, CAST_SPLIT:], src[:, CAST_SPLIT:])
+        nc.vector.tensor_copy(dst[:, :CAST_SPLIT], src[:, :CAST_SPLIT])
+        w1_q = keep.tile([P, H], U32, name="w1_q", align_bytes=64)
         w1_s = keep.tile([P, H], U8, name="w1_s", align_bytes=64)
-        for u in range(2):
+
+        def quantise_w1(u):
             pair = slice(2 * u * P, 2 * (u + 1) * P)
             nc.vector.quantize_mx(
                 w1_q[:, pair].bitcast(FP8X4), w1_s[:, pair],
                 w1_bf[:, 2 * u : 2 * u + 2].rearrange("p t m j -> p (t m j)"),
             )
 
-        w2_raw = keep.tile([P, PACK, N], F32, name="w2_raw", tag="w_raw", align_bytes=64)
+        w2_raw = keep.tile([P, PACK, N], F32, name="w2_raw", tag="d_side", align_bytes=64)
         nc.sync.dma_start(w2_raw[:], w2.rearrange("(p j) c -> p j c", j=PACK))
 
-        x_one = keep.tile([P, S], U32, name="x_one", tag="d_side", align_bytes=64)
+        x_one = keep.tile([P, S], U32, name="x_one", align_bytes=64)
         x_two = keep.tile([P, S], U32, name="x_two", align_bytes=64)
+        quantise_w1(0)
         nc.vector.tensor_copy(x_one[:], xw_win[:].indirect(offs_sb[:]))
+        quantise_w1(1)
         nc.vector.tensor_copy(x_two[:], xw_win[:].indirect(two_sb[:]))
-        dw_win = keep.tile([P, G], U32, name="dw_win", tag="words", align_bytes=64)
-        nc.sync.dma_start(dw_win[:].bitcast(I32), d_words[0].rearrange("p n r -> p (n r)").bitcast(I32))
+        b_s = place_scales(b_got, "b_s", "w1_bf")
+        gn_sb = keep.tile([P, TILES], F32, name="gn_sb", tag="words")
+        nc.sync.dma_start(gn_sb[:], gn.rearrange("(p t) o -> p (t o)", t=TILES))
 
-        y_ps, y_sb, y_got, st, th = [], [], [], [], []
+        y_ps = []
         for t in range(TILES):
             y_ps.append(psum.tile([P, S], F32, name=f"y_ps{t}", tag=f"bank{t}"))
             nc.tensor.matmul_mx(
                 y_ps[t][:], lhsT=w1_q[:, block(t)].bitcast(FP8X4), lhsT_scale=w1_s[:, block(t)],
                 rhs=x_one[:].bitcast(FP8X4), rhs_scale=one_s[:], start=True, stop=True,
             )
-            y_sb.append(keep.tile([P, S], F32, name=f"y_sb{t}"))
             if t == 0:
-                nc.scalar.copy(y_sb[t][:], y_ps[t][:])
+                nc.scalar.copy(rows[t][:, :S], y_ps[t][:])
             else:
-                nc.vector.tensor_copy(y_sb[t][:], y_ps[t][:])
+                nc.vector.tensor_copy(rows[t][:, :S], y_ps[t][:])
+        d_got = keep.tile([P, H], U32, name="d_got", align_bytes=64)
+        nc.vector.tensor_copy(d_got[:], dw_win[:].indirect(k1_sb[:]))
+        st = keep.tile([P, TILES, S], F32, name="st", tag="x_side", align_bytes=64)
         for t in range(TILES):
-            y_got.append(keep.tile([P, S], F32, name=f"y_got{t}"))
-            for h in range(2):
-                nc.scalar.activation(y_got[t][:, cols(h)], y_sb[t][:].indirect(half_of(n1_sb, h)), ACT.Copy)
-            st.append(keep.tile([P, S], F32, name=f"st{t}"))
-            nc.vector.tensor_tensor(st[t][:], y_ps[t][:], y_got[t][:], ALU.add)
+            y_got = keep.tile([P, S], F32, name=f"y_got{t}")
+            nc.scalar.activation(y_got[:], rows[t][:].indirect(n1_sb[:]), ACT.Copy)
+            nc.vector.tensor_tensor(st[:, t, :], y_ps[t][:], y_got[:], ALU.add)
         for t in range(TILES):
-            th.append(keep.tile([P, S], F32, name=f"th{t}"))
-            nc.scalar.activation(th[t][:], st[t][:], ACT.Tanh)
+            nc.scalar.activation(rows[t][:, :S], st[:, t, :], ACT.Tanh)
+
+        b_ps = [psum.tile([P, 2 * S], F32, name=f"b_ps{u}", tag=f"bank{TILES + u}") for u in range(2)]
+        for t in range(TILES):
+            nc.tensor.matmul_mx(
+                b_ps[t // 2][:, (t % 2) * S : (t % 2 + 1) * S], lhsT=d_got[:, block(t)].bitcast(FP8X4),
+                lhsT_scale=b_s[:, S + t * P : S + (t + 1) * P],
+                rhs=x_two[:].bitcast(FP8X4), rhs_scale=b_s[:, 0:S], start=True, stop=True,
+            )
 
         w2_bf = keep.tile([P, N, PACK], BF16, name="w2_bf", tag="w_bf", align_bytes=64)
         nc.vector.tensor_copy(
@@ -133,67 +148,48 @@ def tile_picked_cdjoingatebhopp_none_p_kernel(
         w2_s = keep.tile([P, N], U8, name="w2_s", align_bytes=64)
         nc.vector.quantize_mx(w2_q[:].bitcast(FP8X4), w2_s[:], w2_bf[:].rearrange("p c j -> p (c j)"))
 
-        d_got = keep.tile([P, H], U32, name="d_got", tag="w_bf", align_bytes=64)
-        nc.vector.tensor_copy(d_got[:], dw_win[:].indirect(k1_sb[:]))
-        b_ps = []
+        z_rows = keep.tile([P, TILES, S], BF16, name="z_rows", tag="w_bf", align_bytes=64)
         for t in range(TILES):
-            b_ps.append(psum.tile([P, S], F32, name=f"b_ps{t}", tag=f"bank{TILES + t}"))
-            nc.tensor.matmul_mx(
-                b_ps[t][:], lhsT=d_got[:, block(t)].bitcast(FP8X4),
-                lhsT_scale=b_s[:, S + t * P : S + (t + 1) * P],
-                rhs=x_two[:].bitcast(FP8X4), rhs_scale=b_s[:, 0:S], start=True, stop=True,
+            th_got = keep.tile([P, S], F32, name=f"th_got{t}")
+            nc.scalar.activation(th_got[:], rows[t][:].indirect(n2_sb[:]), ACT.Copy)
+            nc.vector.scalar_tensor_tensor(
+                z_rows[:, t, :], st[:, t, :], gn_sb[:, t : t + 1], th_got[:], ALU.mult, ALU.mult
             )
-
+        z_bf = keep.tile([P, S, PACK], BF16, name="z_bf", align_bytes=64)
+        nc.vector.tensor_copy(
+            z_bf[:].rearrange("p (c i) t -> p c t i", i=4), z_rows[:].rearrange("p t (c i) -> p c t i", i=4)
+        )
+        z_q = keep.tile([P, S], U32, name="z_q", align_bytes=64)
+        z_s = keep.tile([P, S], U8, name="z_s", align_bytes=64)
+        nc.vector.quantize_mx(z_q[:].bitcast(FP8X4), z_s[:], z_bf[:].rearrange("p c t -> p (c t)"))
         a_ps = [psum.tile([P, S], F32, name=f"a_ps{t}", tag=f"bank{t}") for t in range(TILES)]
-        for h in range(2):
-            th_got = keep.tile([P, TILES, HALF], F32, name=f"th_got{h}")
-            z_rows = keep.tile([P, TILES, HALF], BF16, name=f"z_rows{h}", tag=("words", "w_raw")[h], align_bytes=64)
-            for t in range(TILES):
-                nc.scalar.activation(th_got[:, t, :], th[t][:].indirect(half_of(n2_sb, h)), ACT.Copy)
-                nc.vector.scalar_tensor_tensor(
-                    z_rows[:, t, :], st[t][:, cols(h)], gn_sb[:, t : t + 1], th_got[:, t, :], ALU.mult, ALU.mult
-                )
-            z_bf = keep.tile([P, HALF, PACK], BF16, name=f"z_bf{h}", align_bytes=64)
-            nc.vector.tensor_copy(
-                z_bf[:].rearrange("p (c i) t -> p c t i", i=4), z_rows[:].rearrange("p t (c i) -> p c t i", i=4)
-            )
-            z_q = keep.tile([P, HALF], U32, name=f"z_q{h}", align_bytes=64)
-            z_s = keep.tile([P, HALF], U8, name=f"z_s{h}", align_bytes=64)
-            nc.vector.quantize_mx(z_q[:].bitcast(FP8X4), z_s[:], z_bf[:].rearrange("p c t -> p (c t)"))
-            for t in range(TILES):
-                nc.tensor.matmul_mx(
-                    a_ps[t][:, cols(h)], lhsT=w2_q[:, block(t)].bitcast(FP8X4), lhsT_scale=w2_s[:, block(t)],
-                    rhs=z_q[:].bitcast(FP8X4), rhs_scale=z_s[:], start=True, stop=True,
-                )
-
-        gate = []
-        tb = []
         for t in range(TILES):
-            tb.append(keep.tile([P, S], F32, name=f"tb{t}"))
-            nc.scalar.activation(tb[t][:], b_ps[t][:], ACT.Tanh, scale=0.0625 * 0.5)
+            nc.tensor.matmul_mx(
+                a_ps[t][:], lhsT=w2_q[:, block(t)].bitcast(FP8X4), lhsT_scale=w2_s[:, block(t)],
+                rhs=z_q[:].bitcast(FP8X4), rhs_scale=z_s[:], start=True, stop=True,
+            )
+
+        for t in range(TILES):
+            nc.scalar.activation(
+                rows[t][:, S : 2 * S], b_ps[t // 2][:, (t % 2) * S : (t % 2 + 1) * S], ACT.Tanh, scale=0.0625 * 0.5
+            )
+        gate = []
         for t in range(TILES):
             gate.append(keep.tile([P, S], F32, name=f"gate{t}"))
-            for h in range(2):
-                nc.scalar.activation(gate[t][:, cols(h)], tb[t][:].indirect(half_of(n4_sb, h)), ACT.Copy)
+            nc.scalar.activation(gate[t][:], rows[t][:, S:].indirect(n4_sb[:]), ACT.Copy)
 
-        nhs = []
         for t in range(TILES):
-            nhs.append(keep.tile([P, S], F32, name=f"nh{t}"))
-            nc.vector.tensor_scalar(nhs[t][:], a_ps[t][:], -0.5, None, ALU.mult)
+            nc.vector.tensor_scalar(rows[t][:, :S], a_ps[t][:], -0.5, None, ALU.mult)
+        res, prod = [], []
         for t in range(TILES):
-            nh = nhs[t]
-            prod = keep.tile([P, S], F32, name=f"prod{t}")
-            nc.vector.scalar_tensor_tensor(prod[:], gate[t][:], 1.0, nh[:], ALU.add, ALU.mult)
-            res = keep.tile([P, S], F32, name=f"res{t}")
+            prod.append(keep.tile([P, S], F32, name=f"prod{t}"))
+            nc.vector.scalar_tensor_tensor(prod[t][:], gate[t][:], 1.0, rows[t][:, :S], ALU.add, ALU.mult)
+            res.append(keep.tile([P, S], F32, name=f"res{t}"))
+            if t < FUSED_TILES:
+                nc.vector.tensor_tensor(res[t][:], rows[t][:].indirect(n3_sb[:]), prod[t][:], ALU.subtract)
+                nc.sync.dma_start(out[block(t), :], res[t][:])
+        for t in range(FUSED_TILES, TILES):
             got = keep.tile([P, S], F32, name=f"a_got{t}")
-            fused = min(max(FUSED_HALVES - 2 * t, 0), 2)
-            for h in range(fused):
-                nc.vector.tensor_tensor(
-                    res[:, cols(h)], nh[:].indirect(half_of(n3_sb, h)), prod[:, cols(h)], ALU.subtract
-                )
-            for h in range(fused, 2):
-                nc.scalar.activation(got[:, cols(h)], nh[:].indirect(half_of(n3_sb, h)), ACT.Copy)
-            if fused < 2:
-                rest = slice(fused * HALF, S)
-                nc.vector.tensor_tensor(res[:, rest], got[:, rest], prod[:, rest], ALU.subtract)
-            nc.sync.dma_start(out[block(t), :], res[:])
+            nc.scalar.activation(got[:], rows[t][:].indirect(n3_sb[:]), ACT.Copy)
+            nc.vector.tensor_tensor(res[t][:], got[:], prod[t][:], ALU.subtract)
+            nc.sync.dma_start(out[block(t), :], res[t][:])

@@ -18,8 +18,9 @@ ALU = mybir.AluOpType
 P = 128
 PACK = 4
 TILES = 4
+HALF = S // 2
 FUSED_TILES = 1
-CAST_SPLIT = 56
+CAST_SPLIT = 32
 
 
 def tile_picked_cdjoingatebhopp_none_p_kernel(
@@ -41,17 +42,17 @@ def tile_picked_cdjoingatebhopp_none_p_kernel(
         def as_words(packed):
             return packed[0].rearrange("p n r -> p (n r)").bitcast(I32)
 
-        xs_win = keep.tile([P, T], U8, name="xs_win", tag="x_side", align_bytes=64)
+        xs_win = keep.tile([P, T], U8, name="xs_win")
         ds_win = keep.tile([P, G], U8, name="ds_win", tag="d_side", align_bytes=64)
         nc.vector.memset(xs_win[:].bitcast(I32), 0)
         nc.gpsimd.memset(ds_win[:].bitcast(I32), 0)
         rows = [keep.tile([P, 3 * S], F32, name=f"rows{t}") for t in range(TILES)]
         for t in range(TILES - 1):
-            nc.gpsimd.memset(rows[t][:, S:], 0.0)
+            nc.vector.memset(rows[t][:, S:], 0.0)
         nc.scalar.copy(rows[TILES - 1][:, S:], rows[0][:, S:])
 
         offs_sb = load_list(offs, "offs_sb")
-        w1_raw = keep.tile([P, PACK, H], F32, name="w1_raw")
+        w1_raw = keep.tile([P, PACK, H], F32, name="w1_raw", tag="w_raw")
         w1_rows = w1.rearrange("(p j) c -> p j c", j=PACK)
         nc.sync.dma_start(w1_raw[:, 0:2, :], w1_rows[:, 0:2, :])
         nc.sync.dma_start(xs_win[0:P:8, :].bitcast(I32), x_scales[0].bitcast(I32))
@@ -79,10 +80,10 @@ def tile_picked_cdjoingatebhopp_none_p_kernel(
         b_got = keep.tile([P, S + H], U8, name="b_got")
         nc.vector.tensor_copy(b_got[:, 0:S], xs_win[:].indirect(two_sb[:]))
 
-        dw_win = keep.tile([P, G], U32, name="dw_win", tag="x_side", align_bytes=64)
+        nc.vector.tensor_copy(b_got[:, S:], ds_win[:].indirect(k1_sb[:]))
+        dw_win = keep.tile([P, G], U32, name="dw_win", tag="d_side", align_bytes=64)
         nc.sync.dma_start(dw_win[:].bitcast(I32), as_words(d_words))
 
-        nc.vector.tensor_copy(b_got[:, S:], ds_win[:].indirect(k1_sb[:]))
         w1_bf = keep.tile([P, TILES, P, PACK], BF16, name="w1_bf", tag="w1_bf", align_bytes=64)
         src = w1_raw[:].rearrange("p j (m t) -> p m t j", t=TILES)
         dst = w1_bf[:].rearrange("p t m j -> p m t j")
@@ -98,7 +99,7 @@ def tile_picked_cdjoingatebhopp_none_p_kernel(
                 w1_bf[:, 2 * u : 2 * u + 2].rearrange("p t m j -> p (t m j)"),
             )
 
-        w2_raw = keep.tile([P, PACK, N], F32, name="w2_raw", tag="d_side", align_bytes=64)
+        w2_raw = keep.tile([P, PACK, N], F32, name="w2_raw", tag="w_raw")
         nc.sync.dma_start(w2_raw[:], w2.rearrange("(p j) c -> p j c", j=PACK))
 
         x_one = keep.tile([P, S], U32, name="x_one", align_bytes=64)
@@ -124,7 +125,7 @@ def tile_picked_cdjoingatebhopp_none_p_kernel(
                 nc.vector.tensor_copy(rows[t][:, :S], y_ps[t][:])
         d_got = keep.tile([P, H], U32, name="d_got", align_bytes=64)
         nc.vector.tensor_copy(d_got[:], dw_win[:].indirect(k1_sb[:]))
-        st = keep.tile([P, TILES, S], F32, name="st", tag="x_side", align_bytes=64)
+        st = keep.tile([P, TILES, S], F32, name="st", tag="d_side", align_bytes=64)
         for t in range(TILES):
             y_got = keep.tile([P, S], F32, name=f"y_got{t}")
             nc.scalar.activation(y_got[:], rows[t][:].indirect(n1_sb[:]), ACT.Copy)
@@ -156,18 +157,25 @@ def tile_picked_cdjoingatebhopp_none_p_kernel(
                 z_rows[:, t, :], st[:, t, :], gn_sb[:, t : t + 1], th_got[:], ALU.mult, ALU.mult
             )
         z_bf = keep.tile([P, S, PACK], BF16, name="z_bf", align_bytes=64)
-        nc.vector.tensor_copy(
-            z_bf[:].rearrange("p (c i) t -> p c t i", i=4), z_rows[:].rearrange("p t (c i) -> p c t i", i=4)
-        )
         z_q = keep.tile([P, S], U32, name="z_q", align_bytes=64)
         z_s = keep.tile([P, S], U8, name="z_s", align_bytes=64)
-        nc.vector.quantize_mx(z_q[:].bitcast(FP8X4), z_s[:], z_bf[:].rearrange("p c t -> p (c t)"))
+        halves = [slice(h * HALF, (h + 1) * HALF) for h in range(2)]
+        for half in halves:
+            nc.vector.tensor_copy(
+                z_bf[:, half, :].rearrange("p (c i) t -> p c t i", i=4),
+                z_rows[:, :, half].rearrange("p t (c i) -> p c t i", i=4),
+            )
+        for half in halves:
+            nc.vector.quantize_mx(
+                z_q[:, half].bitcast(FP8X4), z_s[:, half], z_bf[:, half, :].rearrange("p c t -> p (c t)")
+            )
         a_ps = [psum.tile([P, S], F32, name=f"a_ps{t}", tag=f"bank{t}") for t in range(TILES)]
         for t in range(TILES):
-            nc.tensor.matmul_mx(
-                a_ps[t][:], lhsT=w2_q[:, block(t)].bitcast(FP8X4), lhsT_scale=w2_s[:, block(t)],
-                rhs=z_q[:].bitcast(FP8X4), rhs_scale=z_s[:], start=True, stop=True,
-            )
+            for half in halves:
+                nc.tensor.matmul_mx(
+                    a_ps[t][:, half], lhsT=w2_q[:, block(t)].bitcast(FP8X4), lhsT_scale=w2_s[:, block(t)],
+                    rhs=z_q[:, half].bitcast(FP8X4), rhs_scale=z_s[:, half], start=True, stop=True,
+                )
 
         for t in range(TILES):
             nc.scalar.activation(

from contextlib import ExitStack

import concourse.mybir as mybir

K, T, S, N, H, G = 512, 2048, 256, 512, 512, 2048
FLOPS = 2 * K * H * S + 2 * H * N * S + 2 * K * H * S

F32 = mybir.dt.float32
BF16 = mybir.dt.bfloat16
I32 = mybir.dt.int32
U32 = mybir.dt.uint32
U16 = mybir.dt.uint16
U8 = mybir.dt.uint8
FP8X4 = mybir.dt.float8_e4m3fn_x4
ACT = mybir.ActivationFunctionType
ALU = mybir.AluOpType

P = 128
PACK = 4
TILES = 4
HALF = S // 2
FUSED_TILES = 1
CAST_SPLIT = 32


def tile_picked_cdjoingatebhopp_none_p_kernel(
    tc, x_words, x_scales, w1, gn, w2, d_words, d_scales, offs, n1, n2, two, k1, n3, n4, out
):
    nc = tc.nc
    with ExitStack() as ctx:
        keep = ctx.enter_context(tc.tile_pool(name="keep", bufs=1))
        psum = ctx.enter_context(tc.psum_pool(name="psum", bufs=1))

        def load_list(src, name):
            tile = keep.tile(list(src.shape), U16, name=name)
            nc.sync.dma_start(tile[:], src)
            return tile

        def block(t):
            return slice(t * P, (t + 1) * P)

        def as_words(packed):
            return packed[0].rearrange("p n r -> p (n r)").bitcast(I32)

        xs_win = keep.tile([P, T], U8, name="xs_win")
        ds_win = keep.tile([P, G], U8, name="ds_win", tag="d_side", align_bytes=64)
        nc.vector.memset(xs_win[:].bitcast(I32), 0)
        nc.gpsimd.memset(ds_win[:].bitcast(I32), 0)
        rows = [keep.tile([P, 3 * S], F32, name=f"rows{t}") for t in range(TILES)]
        for t in range(TILES - 1):
            nc.vector.memset(rows[t][:, S:], 0.0)
        nc.scalar.copy(rows[TILES - 1][:, S:], rows[0][:, S:])

        offs_sb = load_list(offs, "offs_sb")
        w1_raw = keep.tile([P, PACK, H], F32, name="w1_raw", tag="w_raw")
        w1_rows = w1.rearrange("(p j) c -> p j c", j=PACK)
        nc.sync.dma_start(w1_raw[:, 0:2, :], w1_rows[:, 0:2, :])
        nc.sync.dma_start(xs_win[0:P:8, :].bitcast(I32), x_scales[0].bitcast(I32))
        nc.sync.dma_start(ds_win[0:P:8, :].bitcast(I32), d_scales[0].bitcast(I32))
        two_sb = load_list(two, "two_sb")
        k1_sb = load_list(k1, "k1_sb")
        n1_sb = load_list(n1, "n1_sb")
        nc.sync.dma_start(w1_raw[:, 2:4, :], w1_rows[:, 2:4, :])
        xw_win = keep.tile([P, T], U32, name="xw_win", tag="words")
        nc.sync.dma_start(xw_win[:].bitcast(I32), as_words(x_words))
        n2_sb = load_list(n2, "n2_sb")
        n4_sb = load_list(n4, "n4_sb")
        n3_sb = load_list(n3, "n3_sb")

        def place_scales(got, name, tag):
            plane = keep.tile(list(got.shape), U8, name=name, tag=tag, align_bytes=64)
            nc.vector.tensor_copy(plane[:].bitcast(I32), got[:].bitcast(I32))
            for r in range(1, 4):
                nc.sync.dma_start(plane[r:P:32, :].bitcast(I32), got[8 * r : P : 32, :].bitcast(I32))
            return plane

        one_got = keep.tile([P, S], U8, name="one_got")
        nc.vector.tensor_copy(one_got[:], xs_win[:].indirect(offs_sb[:]))
        one_s = place_scales(one_got, "one_s", "one_s")
        b_got = keep.tile([P, S + H], U8, name="b_got")
        nc.vector.tensor_copy(b_got[:, 0:S], xs_win[:].indirect(two_sb[:]))

        nc.vector.tensor_copy(b_got[:, S:], ds_win[:].indirect(k1_sb[:]))
        dw_win = keep.tile([P, G], U32, name="dw_win", tag="d_side", align_bytes=64)
        nc.sync.dma_start(dw_win[:].bitcast(I32), as_words(d_words))

        w1_bf = keep.tile([P, TILES, P, PACK], BF16, name="w1_bf", tag="w1_bf", align_bytes=64)
        src = w1_raw[:].rearrange("p j (m t) -> p m t j", t=TILES)
        dst = w1_bf[:].rearrange("p t m j -> p m t j")
        nc.scalar.copy(dst[:, CAST_SPLIT:], src[:, CAST_SPLIT:])
        nc.vector.tensor_copy(dst[:, :CAST_SPLIT], src[:, :CAST_SPLIT])
        w1_q = keep.tile([P, H], U32, name="w1_q", align_bytes=64)
        w1_s = keep.tile([P, H], U8, name="w1_s", align_bytes=64)

        def quantise_w1(u):
            pair = slice(2 * u * P, 2 * (u + 1) * P)
            nc.vector.quantize_mx(
                w1_q[:, pair].bitcast(FP8X4), w1_s[:, pair],
                w1_bf[:, 2 * u : 2 * u + 2].rearrange("p t m j -> p (t m j)"),
            )

        w2_raw = keep.tile([P, PACK, N], F32, name="w2_raw", tag="w_raw")
        nc.sync.dma_start(w2_raw[:], w2.rearrange("(p j) c -> p j c", j=PACK))

        x_one = keep.tile([P, S], U32, name="x_one", align_bytes=64)
        x_two = keep.tile([P, S], U32, name="x_two", align_bytes=64)
        quantise_w1(0)
        nc.vector.tensor_copy(x_one[:], xw_win[:].indirect(offs_sb[:]))
        quantise_w1(1)
        nc.vector.tensor_copy(x_two[:], xw_win[:].indirect(two_sb[:]))
        b_s = place_scales(b_got, "b_s", "w1_bf")
        gn_sb = keep.tile([P, TILES], F32, name="gn_sb", tag="words")
        nc.sync.dma_start(gn_sb[:], gn.rearrange("(p t) o -> p (t o)", t=TILES))

        y_ps = []
        for t in range(TILES):
            y_ps.append(psum.tile([P, S], F32, name=f"y_ps{t}", tag=f"bank{t}"))
            nc.tensor.matmul_mx(
                y_ps[t][:], lhsT=w1_q[:, block(t)].bitcast(FP8X4), lhsT_scale=w1_s[:, block(t)],
                rhs=x_one[:].bitcast(FP8X4), rhs_scale=one_s[:], start=True, stop=True,
            )
            if t == 0:
                nc.scalar.copy(rows[t][:, :S], y_ps[t][:])
            else:
                nc.vector.tensor_copy(rows[t][:, :S], y_ps[t][:])
        d_got = keep.tile([P, H], U32, name="d_got", align_bytes=64)
        nc.vector.tensor_copy(d_got[:], dw_win[:].indirect(k1_sb[:]))
        st = keep.tile([P, TILES, S], F32, name="st", tag="d_side", align_bytes=64)
        for t in range(TILES):
            y_got = keep.tile([P, S], F32, name=f"y_got{t}")
            nc.scalar.activation(y_got[:], rows[t][:].indirect(n1_sb[:]), ACT.Copy)
            nc.vector.tensor_tensor(st[:, t, :], y_ps[t][:], y_got[:], ALU.add)
        for t in range(TILES):
            nc.scalar.activation(rows[t][:, :S], st[:, t, :], ACT.Tanh)

        b_ps = [psum.tile([P, 2 * S], F32, name=f"b_ps{u}", tag=f"bank{TILES + u}") for u in range(2)]
        for t in range(TILES):
            nc.tensor.matmul_mx(
                b_ps[t // 2][:, (t % 2) * S : (t % 2 + 1) * S], lhsT=d_got[:, block(t)].bitcast(FP8X4),
                lhsT_scale=b_s[:, S + t * P : S + (t + 1) * P],
                rhs=x_two[:].bitcast(FP8X4), rhs_scale=b_s[:, 0:S], start=True, stop=True,
            )

        w2_bf = keep.tile([P, N, PACK], BF16, name="w2_bf", tag="w_bf", align_bytes=64)
        nc.vector.tensor_copy(
            w2_bf[:].rearrange("p (c i) j -> p c j i", i=4), w2_raw[:].rearrange("p j (c i) -> p c j i", i=4)
        )
        w2_q = keep.tile([P, N], U32, name="w2_q", align_bytes=64)
        w2_s = keep.tile([P, N], U8, name="w2_s", align_bytes=64)
        nc.vector.quantize_mx(w2_q[:].bitcast(FP8X4), w2_s[:], w2_bf[:].rearrange("p c j -> p (c j)"))

        z_rows = keep.tile([P, TILES, S], BF16, name="z_rows", tag="w_bf", align_bytes=64)
        for t in range(TILES):
            th_got = keep.tile([P, S], F32, name=f"th_got{t}")
            nc.scalar.activation(th_got[:], rows[t][:].indirect(n2_sb[:]), ACT.Copy)
            nc.vector.scalar_tensor_tensor(
                z_rows[:, t, :], st[:, t, :], gn_sb[:, t : t + 1], th_got[:], ALU.mult, ALU.mult
            )
        z_bf = keep.tile([P, S, PACK], BF16, name="z_bf", align_bytes=64)
        z_q = keep.tile([P, S], U32, name="z_q", align_bytes=64)
        z_s = keep.tile([P, S], U8, name="z_s", align_bytes=64)
        halves = [slice(h * HALF, (h + 1) * HALF) for h in range(2)]
        for half in halves:
            nc.vector.tensor_copy(
                z_bf[:, half, :].rearrange("p (c i) t -> p c t i", i=4),
                z_rows[:, :, half].rearrange("p t (c i) -> p c t i", i=4),
            )
        for half in halves:
            nc.vector.quantize_mx(
                z_q[:, half].bitcast(FP8X4), z_s[:, half], z_bf[:, half, :].rearrange("p c t -> p (c t)")
            )
        a_ps = [psum.tile([P, S], F32, name=f"a_ps{t}", tag=f"bank{t}") for t in range(TILES)]
        for t in range(TILES):
            for half in halves:
                nc.tensor.matmul_mx(
                    a_ps[t][:, half], lhsT=w2_q[:, block(t)].bitcast(FP8X4), lhsT_scale=w2_s[:, block(t)],
                    rhs=z_q[:, half].bitcast(FP8X4), rhs_scale=z_s[:, half], start=True, stop=True,
                )

        for t in range(TILES):
            nc.scalar.activation(
                rows[t][:, S : 2 * S], b_ps[t // 2][:, (t % 2) * S : (t % 2 + 1) * S], ACT.Tanh, scale=0.0625 * 0.5
            )
        gate = []
        for t in range(TILES):
            gate.append(keep.tile([P, S], F32, name=f"gate{t}"))
            nc.scalar.activation(gate[t][:], rows[t][:, S:].indirect(n4_sb[:]), ACT.Copy)

        for t in range(TILES):
            nc.vector.tensor_scalar(rows[t][:, :S], a_ps[t][:], -0.5, None, ALU.mult)
        res, prod = [], []
        for t in range(TILES):
            prod.append(keep.tile([P, S], F32, name=f"prod{t}"))
            nc.vector.scalar_tensor_tensor(prod[t][:], gate[t][:], 1.0, rows[t][:, :S], ALU.add, ALU.mult)
            res.append(keep.tile([P, S], F32, name=f"res{t}"))
            if t < FUSED_TILES:
                nc.vector.tensor_tensor(res[t][:], rows[t][:].indirect(n3_sb[:]), prod[t][:], ALU.subtract)
                nc.sync.dma_start(out[block(t), :], res[t][:])
        for t in range(FUSED_TILES, TILES):
            got = keep.tile([P, S], F32, name=f"a_got{t}")
            nc.scalar.activation(got[:], rows[t][:].indirect(n3_sb[:]), ACT.Copy)
            nc.vector.tensor_tensor(res[t][:], got[:], prod[t][:], ALU.subtract)
            nc.sync.dma_start(out[block(t), :], res[t][:])
